import numpy as np, ml_dtypes
CORES = [1,5,17,21,33,37,49,53]
N = 8
BF = ml_dtypes.bfloat16
def gentries(a):
    return np.ascontiguousarray(a.reshape(8, 16, -1).transpose(0, 2, 1)).reshape(8, -1)
def gtable(e):
    e = np.asarray(e); return np.ascontiguousarray(e.reshape(8, -1, 16).transpose(0, 2, 1)).reshape(128, -1).astype(np.int32)
C, L, M, P, CAP, S, Q, RING = 32, 2048, 64, 256, 32, 2, 3, True
Z = 63 * S
def media(rng):
    return rng.integers(0, M, (N, 8, L)), rng.integers(-63, 64, (N, 8, 128 * M))
def zones(rng):
    t = rng.integers(CAP // 2, CAP + 1, (N, 8)); zr = rng.integers(0, t + 1)
    return np.roll(t - zr, 1, axis=0), zr, P - t - np.roll(t, 1, axis=0)
def crowd(rng, zl, zr, ni, near):
    n = zl + zr + ni; x = rng.integers(0, L, (N, 8, P))
    for r in range(N):
        for g in range(8):
            a = (near * rng.random(zl[r, g]) ** 2).astype(np.int64); b = L - 1 - (near * rng.random(zr[r, g]) ** 2).astype(np.int64)
            x[r, g, :n[r, g]] = rng.permutation(np.concatenate([a, b, rng.integers(Z, L - Z, ni[r, g])]))
    return x, n
def names(rng):
    return rng.integers(1, 2 ** 20, (N, 8, P)) * rng.choice(np.array([-1, 1]), (N, 8, P))
def pack(x, v, w, n, med, kick):
    d = {"x": np.stack([gtable(a) for a in x]), "v": np.stack([gtable(a) for a in v]), "w": np.stack([gtable(a) for a in w])}
    d["live"] = np.repeat(n, 16, axis=1)[:, :, None].astype(np.int32); d["med"] = med.astype(np.int32); d["kick"] = kick.astype(np.int32); return d
def plain(rng):
    zl, zr, room = zones(rng); x, n = crowd(rng, zl, zr, rng.integers(room // 3, room + 1), Z)
    return x, rng.integers(-63, 64, (N, 8, P)), names(rng), n
def setup_inputs(rng):
    return pack(*plain(rng), *media(rng))
def setup_inputs_full(rng):
    s = rng.permutation(np.array([1, 1, 1, 1, -1, -1, -1, -1])); right = np.where(s > 0, CAP, 0); left = CAP - right
    zr = np.tile(right, (N, 1)); zl = np.tile(left, (N, 1))
    if not RING:
        zr[N - 1] = 0; zl[0] = 0
    ni = P - zl - zr
    if not RING:
        ni[N - 1] -= right; ni[0] -= left
    x, n = crowd(rng, zl, zr, ni, 63); med, kick = media(rng); b = 63 * (S + 1)
    med[:, :, :b] = M - 1; med[:, :, L - b:] = M - 1
    for g in range(8):
        kick[:, g, 128 * (M - 1):] = 63 * s[g]
    return pack(x, rng.integers(-63, 64, (N, 8, P)), names(rng), n, med, kick)
def setup_inputs_both(rng):
    zl = np.full((N, 8), CAP); zr = np.full((N, 8), CAP)
    if not RING:
        zl[0] = 0; zr[N - 1] = 0
    x, n = crowd(rng, zl, zr, P - zl - zr, 63); med, kick = media(rng); b = 63 * (S + 1); e = 128 * (M - 1)
    med[:, :, :b] = M - 1; med[:, :, L - b:] = M - 1; kick[:, :, e:e + 64] = -63; kick[:, :, e + 64:] = 63
    side = np.where(x < 63, -1, np.where(x >= L - 63, 1, 0)); v = np.where(side == 0, rng.integers(-63, 64, x.shape), 63 * side); w = np.abs(names(rng))
    for r in range(N):
        for g in range(8):
            for s in (-1, 0, 1):
                k = np.flatnonzero(side[r, g] == s); w[r, g, k] = w[r, g, k] * rng.permutation(1 - 2 * (np.arange(k.size) & 1))
    return pack(x, v, w, n, med, kick)
def setup_inputs_empty(rng):
    x, v, w, n = plain(rng); o = rng.permutation(8); keep = rng.random((N, 8)) > 0.4; keep[:, o[2]] = True; n = np.where(keep, n, 0)
    n[:, o[:2]] = 0; n[rng.integers(0, N), o[0]] = 1
    return pack(x, v, w, n, *media(rng))
def setup_inputs_edges(rng):
    x, v, w, n = plain(rng); med, kick = media(rng); far = (x >= Z) & (x < L - Z)
    y = (x & -64) + 63 * rng.integers(0, 2, x.shape); x = np.where(far & (y >= Z) & (y < L - Z), y, x)
    x = np.where(far, x, np.where(x < Z, rng.choice(np.array([0, 0, 1, 62, 63, 64]), x.shape), L - 1 - rng.choice(np.array([0, 0, 1, 62, 63, 64]), x.shape)))
    v = rng.choice(np.array([-63, -1, 0, 1, 63]), v.shape); kick = np.where(rng.random(kick.shape) < 0.75, rng.choice(np.array([-63, -62, -1, 0, 1, 62, 63]), kick.shape), kick)
    s = rng.permutation(np.array([1, 1, 1, -1, -1, -1, 0, 0]))[None, :, None]; w = np.where(s == 0, w, np.abs(w) * s)
    return pack(x, v, w, n, med, kick)
def setup_inputs_spread(rng):
    zl, zr, room = zones(rng); x, n = crowd(rng, zl, zr, np.maximum(1, (room * rng.random((N, 8)) ** 4).astype(np.int64)), Z)
    w = np.minimum(np.exp2(20 * rng.random((N, 8, P))).astype(np.int64), 2 ** 20 - 1) * rng.choice(np.array([-1, 1]), (N, 8, P))
    v = np.rint(63 * (2 * rng.random((N, 8, P)) - 1) ** 5).astype(np.int64)
    med = np.repeat((M * rng.random((N, 8, L // 16)) ** 3).astype(np.int64), 16, axis=2); kick = np.rint(63 * (2 * rng.random((N, 8, 128 * M)) - 1) ** 3).astype(np.int64)
    return pack(x, v, w, n, med, kick)
def run(x, v, w, n, med, kick):
    worst, most = 0, int(n.max()); ri, gi = np.arange(N)[:, None, None], np.arange(8)[None, :, None]; sh = np.array([[L], [0], [0]])
    for s in range(S):
        on = np.arange(P) < n[:, :, None]; c = x >> 6
        ch = np.zeros((N, 8, C), np.int64); np.add.at(ch, (ri, gi, c), np.where(on, np.sign(w), 0))
        E = np.add.accumulate(ch.transpose(1, 0, 2).reshape(8, N * C), axis=1).reshape(8, N, C).transpose(1, 0, 2)
        u = np.clip(v + np.take_along_axis(E, c, axis=2), -63, 63)
        for i in range(Q):
            m = np.take_along_axis(med, (x + u) & (L - 1), axis=2); u = np.take_along_axis(kick, 128 * m + 64 + u, axis=2)
        x = x + u; v = u
        if not RING:
            k = x[0] < 0; x[0] = np.where(k, -1 - x[0], x[0]); v[0] = np.where(k, -v[0], v[0])
            k = x[N - 1] >= L; x[N - 1] = np.where(k, 2 * L - 1 - x[N - 1], x[N - 1]); v[N - 1] = np.where(k, -v[N - 1], v[N - 1])
        lf, rt = on & (x < 0), on & (x >= L); st = on & ~lf & ~rt
        worst = max(worst, int(np.sum(lf, axis=2).max()), int(np.sum(rt, axis=2).max()))
        t = np.stack([x, v, w]); new = np.zeros((3, N, 8, P), np.int64); cnt = np.zeros((N, 8), np.int64)
        for r in range(N):
            a, b = (r + N - 1) % N, (r + 1) % N
            for g in range(8):
                e = np.concatenate([t[:, r, g][:, st[r, g]], t[:, a, g][:, rt[a, g]] - sh, t[:, b, g][:, lf[b, g]] + sh], axis=1)
                most = max(most, e.shape[1]); cnt[r, g] = min(e.shape[1], P); new[:, r, g, :cnt[r, g]] = e[:, :P]
        x, v, w = new; n = cnt
    return x, v, w, worst, most
def state(x, v, w, live, med, kick):
    h = [np.stack([gentries(a) for a in z]).astype(np.int64) for z in (x, v, w)]
    return h + [live[:, ::16, 0].astype(np.int64), med.astype(np.int64), kick.astype(np.int64)]
def check_inputs(d):
    big = 2 ** 20 - 1
    bad = [k for k, lo, hi in (("x", 0, L - 1), ("v", -63, 63), ("w", -big, big), ("live", 0, P), ("med", 0, M - 1), ("kick", -63, 63)) if d[k].min() < lo or d[k].max() > hi]
    if (d["w"] == 0).any():
        bad.append("w")
    if (d["live"].reshape(N, 8, 16) != d["live"].reshape(N, 8, 16)[:, :, :1]).any():
        bad.append("live")
    if bad:
        return bad
    worst, most = run(*state(d["x"], d["v"], d["w"], d["live"], d["med"], d["kick"]))[3:]
    return (["leavers"] if worst > CAP else []) + (["places"] if most > P else [])
def reference(x, v, w, live, med, kick):
    xe, ve, we, worst, most = run(*state(x, v, w, live, med, kick))
    return {"yx": np.stack([gtable(a) for a in xe]).astype(np.float32), "yv": np.stack([gtable(a) for a in ve]).astype(np.float32), "yw": np.stack([gtable(a) for a in we]).astype(np.float32)}

@@ -1,0 +1,666 @@
+from concourse.bass import DstId, RemoteDMATransfer
+from concourse.mybir import AluOpType as OP, AxisListType as AX, ActivationFunctionType as AF
+
+POOL = {"pf": ("float32", 9000), "pb": ("bfloat16", 24000), "pi": ("int32", 1600), "pu": ("uint16", 640)}
+BANKS = ["U0", "U1", "Y0", "Y1", "Z0", "Z1", "QQ", "MM"]
+SCRATCH = {k: ("sbuf", [128, n], d) for k, (d, n) in POOL.items()}
+SCRATCH.update({b: ("psum", [128, 512], "float32") for b in BANKS})
+NDMA = 12
+SEMAPHORES = ["sV", "sS", "sP", "sG", "loc", "r1", "e0", "e7", "eR", "dL1", "dR1", "n2", "dL2", "dR2"] + \
+             ["dm%d" % i for i in range(NDMA)]
+
+BIGA, BIGB = 8192.0, 32768.0
+SYNC, T_DMA, T_REM, T_CALL = 90.0, 2000.0, 2300.0, 600.0
+CYC, PCYC, TRIES = 1.0, 0.7, 24
+BOOST, BK, BZ, K0 = 2500.0, 1000.0, 0.0, 12
+KS = (3, 3)
+
+
+def build(rank, n, cores, T, topo):
+    ops = []
+    top = {k: 0 for k in POOL}
+
+    def new(pool, w):
+        a = top[pool]
+        top[pool] = a + (w + 15) // 16 * 16
+        assert top[pool] <= POOL[pool][1], pool
+        return (pool, a, a + w, 1)
+
+    def sl(r, a, b=None, s=1):
+        b = a + 1 if b is None else b
+        return (r[0], r[1] + a * r[3], r[1] + (b - 1) * r[3] + 1, s * r[3])
+
+    def wid(r):
+        return (r[2] - r[1] + r[3] - 1) // r[3]
+
+    def ap(r):
+        if not isinstance(r, tuple):
+            return r
+        return T[r[0]][:, r[1]:r[2]] if r[3] == 1 else T[r[0]][:, r[1]:r[2]:r[3]]
+
+    def bank(b, a, c):
+        return (b, a, c, 1)
+
+    def add(eng, fn, rd, wr, dur, **kw):
+        o = dict(eng=eng, fn=fn, rd=[r for r in rd if isinstance(r, tuple)], wr=wr, dur=dur, id=len(ops))
+        o.update(kw)
+        ops.append(o)
+        return o
+
+    def two(*rs):
+        return all(r[0] in ("pb", "pu") for r in rs)
+
+    def vd(nel, f=1.0):
+        return max(64.0, nel * f) * CYC
+
+    def gd(nel, base):
+        return base + 1.55 * nel * CYC
+
+    def src(i, ind):
+        return ap(i) if ind is None else ap(i).indirect(ap(ind))
+
+    def ts(out, i, s1, o0, s2=None, o1=None, ind=None):
+        def fn(e):
+            if o1 is None:
+                return e.tensor_scalar(ap(out), src(i, ind), ap(s1), None, o0)
+            return e.tensor_scalar(ap(out), src(i, ind), ap(s1), ap(s2), o0, o1)
+        d = gd(wid(out), 50) if ind else vd(wid(out), 0.5 if two(out, i) else 1.0)
+        add("V", fn, [i, s1, s2, ind], [out], d)
+        return out
+
+    def tt(out, a, b, o, ind=None):
+        d = gd(wid(out), 50) if ind else vd(wid(out), 1.0 if (a[0] in BANKS or b[0] in BANKS) else 2.0)
+        add("V", lambda e: e.tensor_tensor(ap(out), src(a, ind), ap(b), o), [a, b, ind], [out], d)
+        return out
+
+    def cp(out, i, ind=None):
+        d = gd(wid(out), 50) if ind else vd(wid(out), 0.5 if two(out, i) else 1.0)
+        add("V", lambda e: e.tensor_copy(ap(out), src(i, ind)), [i, ind], [out], d)
+        return out
+
+    def scat(win, off, i):
+        add("V", lambda e: e.tensor_copy(ap(win).indirect(ap(off)), ap(i)), [i, off], [win], 50 + 3.5 * wid(i) * CYC)
+
+    def scan(out, a, b, init, o0, o1):
+        add("V", lambda e: e.tensor_tensor_scan(ap(out), ap(a), ap(b), ap(init), o0, o1), [a, b, init], [out],
+            vd(wid(out), 0.5 if two(out, a, b) else 1.0))
+        return out
+
+    def red(out, i):
+        add("V", lambda e: e.tensor_reduce(ap(out), ap(i), AX.X, OP.add), [i], [out], vd(wid(i)))
+        return out
+
+    def mset(out, c):
+        add("V", lambda e: e.memset(ap(out), c), [], [out], vd(wid(out), 0.5 if two(out) else 1.0))
+        return out
+
+    def act(out, i, f, bias=None, scale=None, acc=None, ind=None):
+        def fn(e):
+            kw = {}
+            if bias is not None:
+                kw["bias"] = ap(bias)
+            if scale is not None:
+                kw["scale"] = ap(scale)
+            if acc is not None:
+                kw["accum_out"] = ap(acc)
+            return e.activation(ap(out), src(i, ind), f, **kw)
+        d = gd(wid(out), 65) if ind else vd(wid(out))
+        add("S", fn, [i, bias, scale, ind], [out] + ([acc] if acc else []), d + (25 if acc else 0))
+        return out
+
+    def mul(out, i, s):
+        return act(out, i, AF.Identity, scale=s)
+
+    grp = [0]
+    opened = {}
+
+    def mm(out, l, r, start=True, stop=True):
+        if start:
+            grp[0] += 1
+            opened[out[0]] = grp[0]
+        d = max(64, wid(r)) * (4 if l[0] == "pf" else 1) * PCYC
+        add("P", lambda e: e.matmul(ap(out), ap(l), ap(r), start, stop), [l, r], [out], d, grp=opened[out[0]])
+        return out
+
+    def iota(out, pat, base, cm):
+        if out[0] == "pi":
+            fn = lambda e: e.iota(ap(out), pat, base, cm)
+        else:
+            fn = lambda e: e.iota(ap(out), pat, base, cm, allow_small_or_imprecise_dtypes=True)
+        add("G", fn, [], [out], 130 + 2 * wid(out) * CYC)
+        return out
+
+    def asel(out, i, pat, o, fill, base, cm):
+        add("G", lambda e: e.affine_select(ap(out), ap(i), pat, o, fill, base, cm), [i], [out], 170 + 2 * wid(out) * CYC)
+        return out
+
+    nd = [0]
+
+    def dma(q, out, i, rd, wr, extra=0.0):
+        s = "dm%d" % nd[0]
+        nd[0] += 1
+        return add(q, lambda e: e.dma_start(out, i), rd, wr, 60.0, lat=T_DMA + extra, dsem=s)
+
+    def plan(a, dsts):
+        far = [d for d in dsts if topo.chip(cores[d]) != topo.chip(cores[a])]
+        near = [d for d in dsts if d not in far]
+        other = [d for d in range(n) if topo.chip(cores[d]) != topo.chip(cores[a])][0]
+        leave = topo.engines(cores[a], cores[other])
+        out = []
+        if far:
+            out.append((leave, far))
+        if near:
+            out.append(([x for x in topo.engines(cores[a], cores[near[0]]) if x not in leave], near))
+        return out
+
+    def count(a, dsts):
+        return [len(e) for e, ds in plan(a, dsts) if rank in ds][0]
+
+    nloc = [0]
+
+    def send(data, dsts, where):
+        tr = []
+        for eng, ds in plan(rank, dsts):
+            m = sum(1 << x for x in eng)
+            ids = [DstId(rid=topo.addr(cores[d])[0], pnc=topo.addr(cores[d])[1]) for d in ds]
+            tr.append((ids, m, where(ds[0])[1], [where(d)[0] for d in ds]))
+            nloc[0] += len(eng)
+
+        def fn(e):
+            return e.remote_dma_fused([RemoteDMATransfer(dst_ids=i, dma_engine_mask=m, remote_sem=T.sem[s], srcs=[ap(data)],
+                                                         dsts=[ap(x) for x in ds]) for i, m, s, ds in tr], local_sem=T.sem.loc)
+        return add("G", fn, [data], [("sent",) + data[1:]], T_CALL, remote=True)
+
+    def recv(land, sem, cnt, ready, lat):
+        return add(None, None, [ready, ("sent",) + ready[1:]], [land], lat, rsem=(sem, cnt))
+
+    F, B, I, U = (lambda w: new("pf", w)), (lambda w: new("pb", w)), (lambda w: new("pi", w)), (lambda w: new("pu", w))
+    left, right = (rank + n - 1) % n, (rank + 1) % n
+
+    landq = B(16 * n)
+    lande = F(4)
+    land1 = F(128)
+    landn = B(2)
+    FW = F(712)
+
+    xi, vi, wi, li, medi, kicki, zp = I(16), I(16), I(16), I(1), I(128), I(512), I(256)
+    dma("Y", ap(wi), T.w[:], [], [wi])
+    dma("S", ap(li), T.live[:], [], [li])
+    dma("Y", ap(xi), T.x[:], [], [xi])
+    dma("S", ap(medi), T.med[:], [], [medi], 200)
+    dma("Y", ap(kicki), T.kick[:], [], [kicki], 800)
+    dma("S", ap(vi), T.v[:], [], [vi])
+    mset(zp, 0)
+    for row, t in ((0, T.x), (2, T.w), (3, T.w)):
+        dma("Y", T.pi[row:128:16, zp[1]:zp[2]], t[:], [zp], [("zp%d" % row, 0, 1, 1)])
+
+    pint = iota(I(1), [[1, 1]], 0, 1)
+    rf = cp(F(1), ts(I(1), pint, 15, OP.bitwise_and))
+    g16 = cp(F(1), ts(I(1), pint, 112, OP.bitwise_and))
+    jL = ts(F(20), iota(F(20), [[16, 20]], 0, 1), g16, OP.subtract)
+    c16 = iota(B(128), [[16, 8], [0, 16]], 0, -1)
+    dg = iota(B(128), [[32, 8], [1, 16]], 0, -1)
+    t16 = iota(B(16), [[1, 16]], 0, -1)
+    negr = ts(F(1), rf, -1.0, OP.mult)
+    ng = ts(F(1), g16, -1.0, OP.mult)
+    BO = ts(B(128), c16, negr, OP.is_equal)
+    EQ = ts(F(16), t16, ng, OP.is_equal)
+    Sel = [ts(B(128), c16, float(-r), OP.is_equal) for r in range(16)]
+    ident = ts(B(128), dg, g16, OP.is_equal)
+    Kprev = ts(B(128), dg, ts(F(1), g16, 1.0, OP.add), OP.is_equal, -1.0, OP.mult)
+    Klast = ts(B(128), dg, ts(F(1), g16, -15.0, OP.add), OP.is_equal)
+    Tri = asel(B(128), BO, [[1, 128]], OP.is_ge, 0.0, 0, -1)
+    BOh = mul(B(128), BO, 0.5)
+    S0f = mul(F(128), Sel[0], 1.0)
+    d0a = B(16 * K0)
+    tt(sl(d0a, 0, 16), ts(F(16), t16, ts(F(1), ng, 1.0, OP.add), OP.is_equal, BIGA, OP.mult),
+       ts(F(16), EQ, -4 * BIGA, OP.mult), OP.add)
+    w = 16
+    while w < 16 * K0:
+        k = min(w, 16 * K0 - w)
+        mul(sl(d0a, w, w + k), sl(d0a, 0, k), 1.0)
+        w += k
+    d0b = mul(B(16 * K0), d0a, BIGB / BIGA)
+    nfix = ts(F(1), sl(EQ, 15), BIGB, OP.mult, -BIGB, OP.add)
+    fix64 = ts(F(1), nfix, -1.0, OP.mult, 64.0, OP.add)
+    nfix64 = ts(F(1), nfix, 64.0, OP.add)
+    nfixm = ts(F(1), nfix, -64.0, OP.add)
+    HT = mset(B(224), 0.0)
+    ts(sl(HT, 17, 33), EQ, -1.0, OP.mult)
+    cp(sl(HT, 145, 161), EQ)
+    sbias = ts(F(1), rf, -512.0, OP.mult, 64.0, OP.add)
+    kbias = ts(F(1), sl(EQ, 0), 128.0, OP.mult)
+    jP = ts(F(16), iota(F(16), [[1, 16]], 0, 16), ts(F(1), g16, 16.0, OP.mult), OP.subtract)
+    jPu = cp(U(16), jP)
+    jW = iota(B(256), [[1, 256]], 0, 0)
+    par = iota(B(128), [[0, 64], [-8192, 2]], 4096, 0)
+    parBO = asel(B(128), asel(B(128), par, [[-16, 8], [0, 16]], OP.is_ge, 0.0, 0, 1), [[16, 8], [0, 16]], OP.is_ge, 0.0, 15, -1)
+    e01 = ts(F(1), rf, 2.0, OP.is_lt)
+    LP01 = mul(B(128), parBO, e01)
+    LY = asel(F(128), mul(F(128), parBO, sl(EQ, 4)), [[-16, 8], [0, 16]], OP.not_equal, 1.0, 0, 1)
+    LZ = mul(F(128), ident, tt(F(1), ts(F(1), rf, 4.0, OP.is_lt), sl(EQ, 1), OP.subtract))
+    LQ = mul(F(128), BO, ts(F(1), sl(EQ, 3), 4096.0, OP.mult, sl(EQ, 0), OP.add))
+    LQd = mul(B(128), Sel[0], 16384.0)
+    LZm = asel(B(128), BOh, [[0, 8], [-1, 16]], OP.is_ge, 0.0, 1, 0)
+    S01 = mul(B(128), BO, e01)
+    zbias = ts(F(1), e01, -64.0, OP.mult)
+    qbias = ts(F(1), rf, -2048.0, OP.mult, 6080.5, OP.add)
+    zhi = ts(F(1), sl(EQ, 3), -4194303.0, OP.mult, 4194304.0, OP.add)
+    zlo = ts(F(1), zhi, -1.0, OP.mult)
+    rodd = cp(F(1), ts(I(1), pint, 1, OP.bitwise_and))
+    fsgn = ts(F(1), rodd, 2.0, OP.mult, -1.0, OP.add)
+    fth = ts(F(1), rodd, 2175.0, OP.mult, -63.0, OP.add)
+    rh = cp(F(1), ts(I(1), pint, 15, OP.bitwise_and, 1, OP.arith_shift_right))
+    sk = ts(F(4), sl(jL, 0, 4), rf, OP.subtract)
+    sk = ts(F(4), sk, 0.5, OP.mult, rh, OP.add)
+    skh = ts(F(4), sk, 0.5, OP.add)
+    adj = ts(F(64), sl(par, 0, 64), sl(EQ, 0), OP.mult, 0.5, OP.mult)
+    e164 = ts(F(1), sl(EQ, 1), 64.0, OP.mult)
+
+    def coef(pos, neg):
+        return tt(F(1), tt(F(1), sl(EQ, pos[0]), sl(EQ, pos[1]), OP.add), tt(F(1), sl(EQ, neg[0]), sl(EQ, neg[1]), OP.add), OP.subtract)
+
+    CL = mul(F(128), BOh, coef((1, 3), (0, 5)))
+    CR = mul(F(128), BOh, coef((3, 6), (2, 7)))
+    if rank > 0:
+        CLn = mul(F(128), CL, -1.0)
+    T2 = asel(B(128), asel(B(128), mul(B(128), BO, -1.0), [[-1, 128]], OP.is_gt, 0.0, 0, 1), [[-1, 128]], OP.not_equal, 320.0, 0, 1)
+    mset(sl(FW, 320, 580), 0.0)
+    mset(sl(FW, 708, 712), 0.0)
+    Zs, Fs, offc = [F(322), F(322)], [B(257), B(321)], []
+    for s, (w0, w) in enumerate(((128, 256), (16 * K0, 320))):
+        ts(sl(Zs[s], w, w + 2), sl(adj, 0, 2), -1.0, OP.mult, sl(EQ, 4), OP.add)
+        ts(sl(Fs[s], w), rodd, -128.0, OP.mult, 128.0, OP.add)
+        o = F(4)
+        for k in range(4):
+            mset(sl(o, k), float((w0 if k < KS[0] else 0) + (w + 1 - w0 if k < KS[1] else 0)))
+        offc.append(o)
+
+    nf = cp(F(1), li)
+    on = ts(F(16), sl(jL, 0, 16), nf, OP.is_lt)
+    sg = ts(F(16), wi, -1.0, OP.max, 1.0, OP.min)
+    qb = tt(B(16), on, sg, OP.mult)
+    if rank < n - 1:
+        send(qb, list(range(n - 1, rank, -1)), lambda d: (sl(landq, 16 * rank, 16 * rank + 16), "r1"))
+    pre = None
+    lq = sl(landq, 0, 16 * max(rank, 1))
+    recv(lq, "r1", sum(count(a, list(range(n - 1, a, -1))) for a in range(rank)), qb, T_REM + (700 if rank < n - 1 else 1300))
+
+    medb = ts(B(128), medi, 128.0, OP.mult)
+    MT = B(2304)
+    tb = ["Y0", "Y1", "Z0", "Z1"]
+    for k in range(4):
+        for r in range(4 * k, 4 * k + 4):
+            mm(bank(tb[k], 128 * (r % 4), 128 * (r % 4) + 128), Sel[r], medb)
+            ops[-1]["boost"] = BOOST - 500.0 * k
+        act(sl(MT, 128 + 512 * k, 640 + 512 * k), bank(tb[k], 0, 512), AF.Identity)
+    cp(sl(MT, 0, 128), sl(MT, 2048, 2176))
+    cp(sl(MT, 2176, 2304), sl(MT, 128, 256))
+    kb = cp(B(512), kicki)
+    ops[-1]["boost"] = BK
+    for i, l in enumerate((ident, Kprev, Klast)):
+        mm(bank("QQ", 0, 512), l, kb, i == 0, i == 2)
+    KT = act(B(512), bank("QQ", 0, 512), AF.Identity, bias=kbias)
+
+    def field(ho, q, v):
+        h = F(2)
+        S0 = act(B(256), sl(HT, 16, 224), AF.Identity, acc=sl(h, 0), ind=ho)
+        S1 = act(B(256), sl(HT, 0, 208), AF.Identity, acc=sl(h, 1), ind=ho)
+        hb = cp(B(2), h)
+        mm(bank("MM", 0, 2), Tri, hb, True, False)
+        mm(bank("MM", 1, 2), BO, sl(hb, 0), False, True)
+        l0 = ts(B(128), BO, bank("MM", 0, 1), OP.mult)
+        l1 = ts(B(128), BO, bank("MM", 1, 2), OP.mult)
+        mm(bank("U0", 0, 256), l0, S0, True, False)
+        mm(bank("U0", 0, 256), l1, S1, False, True)
+        sc = F(256)
+        for a in (0, 128):
+            scan(sl(sc, a, a + 128), sl(d0b, 0, 128), bank("U0", a, a + 128), 0.0, OP.add, OP.max)
+        return tt(F(16), tt(F(16), sl(sc, 15, 256, 16), q, OP.mult), v, OP.add), hb
+
+    def start(vE, base, xfix, uo, yo):
+        a = ts(F(wid(vE)), vE, base, OP.add, -63.0, OP.max) if base is not None else ts(F(wid(vE)), vE, -63.0, OP.max)
+        if base is None:
+            ops[-1]["rd"].append(lq)
+        ts(uo, a, 63.0, OP.min, fix64, OP.add)
+        cp(yo, tt(F(wid(vE)), uo, xfix, OP.add))
+
+    def scatter3(b, k, yo, u, x, xw, last):
+        w = 16 * k
+        for it in range(3):
+            mw = act(B(w), MT, AF.Identity, ind=yo)
+            sgn = act(B(w), MT, AF.Sign, bias=sbias, ind=yo)
+            sm = scan(B(w), sl(d0a, 0, w), mw, 0.0, OP.add, OP.max)
+            ko = cp(U(k), ts(I(k), tt(I(k), sl(sm, 15, w, 16), u, OP.add), 511, OP.bitwise_and))
+            kw = tt(B(w), KT, sgn, OP.mult, ind=ko)
+            if it == 2:
+                last(kw)
+                return
+            mm(bank("U%d" % b, 0, w), S0f, xw, True, False)
+            mm(bank("U%d" % b, 0, w), BOh, kw, False, True)
+            su = scan(F(w), sl(d0b, 0, w), bank("U%d" % b, 0, w), 0.0, OP.add, OP.max)
+            yo = ts(U(k), sl(su, 15, w, 16), nfix64, OP.add)
+            u = tt(F(k), sl(su, 15, w, 16), x, OP.subtract)
+
+    def leavers(s, b, c0, w, st):
+        Z, Fl = Zs[s], Fs[s]
+        x = 1 if b else 0
+        ts(sl(Fl, c0, c0 + w), bank("Y%d" % b, 0, w), fsgn, OP.mult, fth, OP.is_ge)
+        cum = sl(st["cum"], c0, c0 + w + x)
+        f = sl(Fl, c0, c0 + w + x)
+        scan(cum, f, f, sl(st["cum"], c0 - 1) if b else 0.0, OP.add, OP.max)
+        act(sl(Z, c0, c0 + w), bank("Z%d" % b, 0, w), AF.Identity, bias=zbias)
+        cnt = F(4)
+        for k in range(4):
+            if k < KS[b]:
+                act(B(w + x), cum, AF.Sign, bias=sl(skh, k), scale=-1.0, acc=sl(cnt, k))
+            else:
+                red(sl(cnt, k), ts(B(w + x), cum, sl(sk, k), OP.is_le, 2.0, OP.mult))
+        if b == 0:
+            st["cnt"] = tt(F(4), cnt, offc[s], OP.add)
+            return None
+        so = ts(U(4), tt(F(4), cnt, st["cnt"], OP.add), 0.5, OP.mult)
+        return tt(F(64), sl(Z, 0, c0 + w + 2), adj, OP.add, ind=so)
+
+    def exchange(msg, s, lL, lR):
+        names = ("dL%d" % s, "dR%d" % s)
+        send(msg, [right, left], lambda d: (lL, names[0]) if d == right else (lR, names[1]))
+        recv(lL, names[0], count(left, [rank, (left + n - 1) % n]), msg, T_REM)
+        recv(lR, names[1], count(right, [(right + 1) % n, rank]), msg, T_REM)
+
+    xf = cp(F(16), xi)
+    ho = cp(U(16), tt(F(16), ts(I(16), xi, 6, OP.arith_shift_right), ts(F(16), qb, 64.0, OP.mult, 65.0, OP.add), OP.add))
+    qfix = ts(F(16), qb, nfix, OP.mult)
+    vE, _ = field(ho, qb, tt(F(16), qfix, vi, OP.add))
+    if rank > 0:
+        mm(bank("U1", 0, 16 * rank), BO, lq)
+        pre = red(F(1), bank("U1", 0, 16 * rank))
+    xfix = ts(F(16), xf, nfix64, OP.add)
+    u0, y0 = F(16), U(16)
+    start(vE, pre, xfix, u0, y0)
+    Z0 = F(256)
+    add("V", lambda e: e.tensor_scalar(ap(Z0), ap(zp).indirect(ap(jPu)), ap(zlo), ap(zhi), OP.max, OP.min),
+        [zp, jPu, zlo, zhi, ("zp0", 0, 1, 1), ("zp2", 0, 1, 1), ("zp3", 0, 1, 1)], [Z0], gd(256, 50), boost=BZ)
+    dead = ts(B(256), jW, nf, OP.is_ge)
+    mm(bank("QQ", 0, 256), LQ, Z0, True, False)
+    mm(bank("QQ", 0, 256), LQd, dead, False, False)
+    st1 = dict(cum=B(257))
+    sy = F(256)
+    msg = [None]
+    for b in range(2):
+        c0 = 128 * b
+        mm(bank("Y%d" % b, 0, 128), LY, sl(Z0, c0, c0 + 128), True, False)
+        mm(bank("Y%d" % b, 0, 128), LP01, sl(dead, c0, c0 + 128), False, False)
+        mm(bank("Z%d" % b, 0, 128), LZ, sl(Z0, c0, c0 + 128), True, False)
+
+        def last(kw, b=b, c0=c0):
+            if b == 1:
+                mm(bank("QQ", c0, c0 + 128), BOh, kw, False, True)
+            mm(bank("Y%d" % b, 0, 128), BOh, kw, False, True)
+            if b == 0:
+                mm(bank("QQ", c0, c0 + 128), BOh, kw, False, False)
+            mm(bank("Z%d" % b, 0, 128), LZm, kw, False, True)
+        scatter3(b, 8, sl(y0, 8 * b, 8 * b + 8), sl(u0, 8 * b, 8 * b + 8), sl(xf, 8 * b, 8 * b + 8), sl(Z0, c0, c0 + 128), last)
+    acc = F(1)
+    act(B(256), bank("QQ", 0, 256), AF.Sign, bias=qbias, acc=acc)
+
+    def edst(a):
+        return [d for d in range(n) if d != a] if a in (0, n - 1) else [a - 1]
+
+    def ecol(a):
+        return (0, "e0") if a == 0 else (1, "e7") if a == n - 1 else (2, "eR")
+    send(acc, edst(rank), lambda d: (sl(lande, ecol(rank)[0]), ecol(rank)[1]))
+    got = {rank: acc}
+    for a in sorted({0, n - 1, right} - {rank}):
+        got[a] = sl(lande, ecol(a)[0])
+        recv(got[a], ecol(a)[1], count(a, edst(a)), acc, T_REM + (700 if a in (0, n - 1) else 0))
+    for b in range(2):
+        msg[0] = leavers(0, b, 128 * b, 128, st1)
+    exchange(msg[0], 1, sl(land1, 0, 64), sl(land1, 64, 128))
+    for b in range(2):
+        scan(sl(sy, 128 * b, 128 * b + 128), sl(d0b, 0, 128), bank("QQ", 128 * b, 128 * b + 128), 0.0, OP.add, OP.max)
+
+    qv = sl(sy, 15, 256, 16)
+    ho = ts(I(16), qv, ts(F(1), nfix, 4096.0, OP.add), OP.add, 12800.0, OP.min)
+    ho = cp(U(16), ts(I(16), ho, 6, OP.arith_shift_right))
+    xx = F(20)
+    yr = tt(sl(xx, 0, 16), qv, ts(F(16), sg, -4096.0, OP.mult, nfixm, OP.add), OP.add)
+    x2 = ts(F(16), yr, 0.0, OP.max, 2047.0, OP.min)
+    v2 = tt(F(16), qfix, xf, OP.subtract)
+    if pre is not None:
+        v2 = ts(F(16), v2, pre, OP.add)
+    e31 = mm(bank("U1", 0, 1), CL, got[right])
+    v2 = tt(F(16), tt(F(16), v2, yr, OP.add), ts(F(16), x2, 1984.0, OP.is_ge, e31, OP.mult), OP.add)
+    vE, hb = field(ho, qb, v2)
+    mm(bank("MM", 2, 3), Sel[0], sl(hb, 0))
+    mm(bank("MM", 3, 4), BO, sl(hb, 0), True, False)
+    mm(bank("MM", 3, 4), BO, sl(hb, 1), False, True)
+    if pre is not None:
+        cs = ts(F(2), bank("MM", 2, 4), pre, OP.add, sl(EQ, 1), OP.mult)
+    else:
+        cs = ts(F(2), bank("MM", 2, 4), sl(EQ, 1), OP.mult)
+    preR = tt(F(1), sl(cs, 1), sl(adj, 1), OP.add)
+    preR = ts(F(1), e31, sl(EQ, 1), OP.mult, preR, OP.add)
+    base = bank("QQ", 0, 1)
+    terms = [(CR, got[n - 1])] if rank == 0 else [(CL, acc), (CR, got[n - 1]), (CLn, got[0])]
+    for i, (l, r) in enumerate(terms):
+        mm(base, l, r, i == 0, i == len(terms) - 1)
+    u0, y0 = F(20), U(20)
+    start(vE, base, ts(F(16), x2, nfix64, OP.add), sl(u0, 0, 16), sl(y0, 0, 16))
+    ab = B(64)
+    Z1 = Zs[0]
+    for side, pr in ((0, sl(cs, 0)), (1, preR)):
+        a = sl(land1, 64 * side + 1 - side, 64 * side + 64, 2)
+        ecolumn = ts(F(1), base, sl(EQ, 1), OP.mult, pr, OP.add)
+        t = ts(F(32), a, ecolumn, OP.add, -63.0, OP.max)
+        ts(sl(ab, 32 * side, 32 * side + 32), t, 63.0, OP.min, e164, OP.add)
+        act(sl(Z1, 256 + 32 * side, 288 + 32 * side), a, AF.Identity)
+    mm(bank("U1", 0, 64), S01, ab)
+    mm(bank("U1", 64, 128), Sel[1], ab)
+    sa = scan(F(128), sl(d0b, 0, 128), bank("U1", 0, 128), 0.0, OP.add, OP.max)
+    ts(sl(y0, 16, 20), sl(sa, 15, 64, 16), nfix64, OP.add)
+    cp(sl(u0, 16, 20), sl(sa, 79, 128, 16))
+    tt(sl(xx, 16, 20), sl(sa, 15, 64, 16), sl(sa, 79, 128, 16), OP.subtract)
+    st2 = dict(cum=B(321))
+    sy = F(320)
+    parts = ((0, K0), (K0, 20))
+    for b, (k0, k1) in enumerate(parts):
+        c0, w = 16 * k0, 16 * (k1 - k0)
+        c1 = min(c0 + w, 256)
+        mm(bank("Y%d" % b, 0, w), LY, sl(Z1, c0, c0 + w), True, False)
+        mm(bank("Y%d" % b, 0, c1 - c0), LP01, sl(dead, c0, c1), False, False)
+        mm(bank("Y%d" % b, 0, c1 - c0), LP01, sl(Fs[0], c0, c1), False, False)
+        mm(bank("Z%d" % b, 0, w), LZ, sl(Z1, c0, c0 + w), True, False)
+
+        def last(kw, b=b, w=w):
+            mm(bank("Y%d" % b, 0, w), BOh, kw, False, True)
+            mm(bank("Z%d" % b, 0, w), LZm, kw, False, True)
+        scatter3(b, k1 - k0, sl(y0, k0, k1), sl(u0, k0, k1), sl(xx, k0, k1), sl(Z1, c0, c0 + w), last)
+    for b, (k0, k1) in enumerate(parts):
+        msg[0] = leavers(1, b, 16 * k0, 16 * (k1 - k0), st2)
+    cnt2 = sl(st2["cum"], 318, 320)
+    send(cnt2, [right], lambda d: (landn, "n2"))
+    recv(landn, "n2", count(left, [rank]), cnt2, T_REM)
+    exchange(msg[0], 2, sl(FW, 580, 644), sl(FW, 644, 708))
+
+    for b, (k0, k1) in enumerate(parts):
+        w = 16 * (k1 - k0)
+        scan(sl(sy, 16 * k0, 16 * k1), sl(d0b, 0, w), bank("Y%d" % b, 0, w), 0.0, OP.add, OP.max)
+    yr = ts(F(20), sl(sy, 15, 320, 16), nfixm, OP.add)
+    stay = tt(B(20), ts(F(20), yr, 0.0, OP.max, 2047.0, OP.min), yr, OP.is_equal)
+    inc = scan(B(20), stay, stay, 0.0, OP.add, OP.max)
+    mm(bank("U0", 0, 20), BO, inc, True, False)
+    mm(bank("U0", 0, 20), T2, stay, False, True)
+    ns = mm(bank("MM", 0, 1), BO, sl(inc, 19))
+    pos = cp(U(20), tt(F(20), bank("U0", 0, 20), jL, OP.max))
+    scat(sl(FW, 0, 577), pos, sl(Zs[1], 0, 320))
+    t = ts(F(16), jP, ns, OP.subtract)
+    A = tt(F(16), ts(F(16), t, 2.0, OP.mult, 261.0, OP.add), ts(F(16), t, 0.0, OP.is_lt, -4096.0, OP.mult), OP.add)
+    j1 = ts(F(16), jP, 1.0, OP.add)
+    nl = mm(bank("U1", 0, 1), Sel[1], sl(landn, 1))
+    s2 = ts(F(1), nl, -2.0, OP.mult, 63.0, OP.add)
+    c = tt(F(16), A, ts(F(16), t, nl, OP.is_ge, s2, OP.mult), OP.add)
+    fo = ts(U(16), tt(F(16), c, j1, OP.max), 388.0, OP.min)
+    FO = F(256)
+    win = sl(FW, 320, 712)
+    cp(sl(FO, 0, 128), win, ind=sl(fo, 0, 8))
+    act(sl(FO, 128, 256), win, AF.Identity, ind=sl(fo, 8, 16))
+    for row, q, t in ((0, "Y", T.yx), (1, "S", T.yv), (2, "Y", T.yw)):
+        dma(q, t[:], T.pf[row:128:16, FO[1]:FO[2]], [FO], [])
+    return ops, nloc[0]
+
+
+def depend(ops):
+    hist = {}
+    for o in ops:
+        d = set()
+        for kind, regs in ((0, o["rd"]), (1, o["wr"])):
+            for r in regs:
+                for (p, k2, a, b) in hist.get(r[0], []):
+                    if p is o:
+                        continue
+                    if r[0] in BANKS:
+                        hit = kind or k2 or p["eng"] != o["eng"]
+                    else:
+                        hit = (kind or k2) and a < r[2] and r[1] < b
+                    if hit:
+                        d.add(p["id"])
+        o["dep"] = d
+        for kind, regs in ((0, o["rd"]), (1, o["wr"])):
+            if o["eng"] is None and kind == 0:
+                continue
+            for r in regs:
+                hist.setdefault(r[0], []).append((o, kind, r[1], r[2]))
+
+
+def loose(p, o):
+    if p["eng"] != "P" or o["eng"] != "P":
+        return False
+    a, b = p["wr"][0], o["wr"][0]
+    return p["grp"] == o["grp"] or a[2] <= b[1] or b[2] <= a[1]
+
+
+def place(ops, key, back):
+    pre, post = ("succ", "dep") if back else ("dep", "succ")
+    busy = {e: [] for e in "VSPGY"}
+    left = [len(o[pre]) for o in ops]
+    start = [0.0] * len(ops)
+    cand = [o["id"] for o in ops if not o[pre]]
+    while cand:
+        i = max(cand, key=lambda j: key[j])
+        cand.remove(i)
+        o = ops[i]
+        if back:
+            t = o["tot"] - o["dur"] + max([start[d] + ops[d]["dur"] - (SYNC if i in ops[d]["loose"] else 0.0) for d in o[pre]] + [0.0])
+        else:
+            t = max([start[d] + ops[d]["tot"] - (SYNC if d in o["loose"] else 0.0) for d in o[pre]] + [0.0])
+        if o["eng"] is not None:
+            l = busy[o["eng"]]
+            k = 0
+            while k < len(l) and l[k][0] < t + o["dur"]:
+                t = max(t, l[k][1])
+                k += 1
+            l.insert(k, (t, t + o["dur"]))
+        start[i] = t
+        for s in o[post]:
+            left[s] -= 1
+            if left[s] == 0:
+                cand.append(s)
+    return start
+
+
+def schedule(ops):
+    for o in ops:
+        o["succ"] = []
+        o["tot"] = o["dur"] + o.get("lat", 0.0) + SYNC
+        o["loose"] = {d for d in o["dep"] if loose(ops[d], o)}
+    for o in ops:
+        for d in o["dep"]:
+            ops[d]["succ"].append(o["id"])
+    for o in reversed(ops):
+        o["pr"] = o["tot"] + o.get("boost", 0.0) + max([ops[s]["pr"] for s in o["succ"]] + [0.0])
+    best, seed = None, 12345
+    for trial in range(TRIES):
+        key = []
+        for o in ops:
+            seed = (seed * 1103515245 + 12345) % 2147483648
+            key.append(o["pr"] + (seed / 2147483648.0) * 100.0 * (trial % 8))
+        for turn in range(4):
+            start = place(ops, key, False)
+            end = [start[o["id"]] + o["tot"] for o in ops]
+            if best is None or max(end) < best[0]:
+                best = (max(end), start, end)
+            rev = place(ops, end, True)
+            key = [rev[o["id"]] + o["dur"] for o in ops]
+    order = {e: [] for e in "VSPGY"}
+    for o in ops:
+        o["start"], o["end"] = best[1][o["id"]], best[2][o["id"]]
+    for o in sorted(ops, key=lambda o: (o["start"], o["id"])):
+        if o["eng"] is not None:
+            order[o["eng"]].append(o)
+    return order
+
+
+def emit(g, T, ops, order, nloc):
+    queue = {"V": g.vector, "S": g.scalar, "P": g.tensor, "G": g, "Y": g.sync}
+
+    def waits_on(o):
+        return [ops[d] for d in o["dep"] if d not in o["loose"] and ops[d].get("rsem", (0, 1))[1] > 0 and not ops[d].get("remote")]
+    seq = sorted([o for o in ops if o["eng"] is not None], key=lambda o: (o["start"], o["id"]))
+    pos = {}
+    for e, l in order.items():
+        for i, o in enumerate(l):
+            pos[o["id"]] = i
+    know = {e: {} for e in order}
+    for o in seq:
+        k = know[o["eng"]]
+        need = []
+        ps = sorted(waits_on(o), key=lambda p: -p["end"])
+        for p in ps:
+            key = p["rsem"][0] if p["eng"] is None else p["dsem"] if "dsem" in p else p["eng"]
+            val = 0 if (p["eng"] is None or "dsem" in p) else pos[p["id"]]
+            if k.get(key, -1) >= val:
+                continue
+            need.append(p)
+            p["inc"] = True
+            k[key] = val
+            for kk, vv in p.get("know", {}).items():
+                if k.get(kk, -1) < vv:
+                    k[kk] = vv
+        o["need"] = need
+        o["know"] = dict(k)
+    for e, l in order.items():
+        c = 0
+        for o in l:
+            if "dsem" not in o and o.get("inc"):
+                c += 1
+                o["val"] = c
+    for o in seq:
+        q = queue[o["eng"]]
+        for p in o["need"]:
+            if p["eng"] is None:
+                q.wait_ge(T.sem[p["rsem"][0]], p["rsem"][1])
+            elif "dsem" in p:
+                q.wait_ge(T.sem[p["dsem"]], 16)
+            else:
+                q.wait_ge(T.sem["s" + p["eng"]], p["val"])
+        ins = o["fn"](q)
+        if "dsem" in o:
+            ins.then_inc(T.sem[o["dsem"]], 16)
+        elif o.get("inc"):
+            ins.then_inc(T.sem["s" + o["eng"]], 1)
+    g.wait_ge(T.sem.loc, nloc)
+    for o in seq:
+        if "dsem" in o and not o.get("inc"):
+            g.wait_ge(T.sem[o["dsem"]], 16)
+
+
+def rank_program(g, core, T, topo):
+    rank = T.rank_of(core)
+    if rank is None:
+        return
+    cores = list(T.cores)
+    ops, nloc = build(rank, len(cores), cores, T, topo)
+    depend(ops)
+    order = schedule(ops)
+    emit(g, T, ops, order, nloc)

@@ -1,7 +1,7 @@
 from concourse.bass import DstId, RemoteDMATransfer
 from concourse.mybir import AluOpType as OP, AxisListType as AX, ActivationFunctionType as AF
 
-POOL = {"pf": ("float32", 9000), "pb": ("bfloat16", 24000), "pi": ("int32", 1600), "pu": ("uint16", 640)}
+POOL = {"pf": ("float32", 11000), "pb": ("bfloat16", 28000), "pi": ("int32", 1600), "pu": ("uint16", 640)}
 BANKS = ["U0", "U1", "Y0", "Y1", "Z0", "Z1", "QQ", "MM"]
 SCRATCH = {k: ("sbuf", [128, n], d) for k, (d, n) in POOL.items()}
 SCRATCH.update({b: ("psum", [128, 512], "float32") for b in BANKS})
@@ -10,9 +10,10 @@ SEMAPHORES = ["sV", "sS", "sP", "sG", "loc", "r1", "e0", "e7", "eR", "dL1", "dR1
              ["dm%d" % i for i in range(NDMA)]
 
 BIGA, BIGB = 8192.0, 32768.0
-SYNC, T_DMA, T_REM, T_CALL = 90.0, 2000.0, 2300.0, 600.0
+SYNC, T_DMA, T_REM, T_CALL = 200.0, 2000.0, 2300.0, 600.0
 CYC, PCYC, TRIES = 1.0, 0.7, 24
 BOOST, BK, BZ, K0 = 2500.0, 1000.0, 0.0, 12
+COPY = "SSSVSSVV"
 KS = (3, 3)
 
 
@@ -222,7 +223,7 @@ def build(rank, n, cores, T, topo):
         w += k
     d0b = mul(B(16 * K0), d0a, BIGB / BIGA)
     nfix = ts(F(1), sl(EQ, 15), BIGB, OP.mult, -BIGB, OP.add)
-    fix64 = ts(F(1), nfix, -1.0, OP.mult, 64.0, OP.add)
+    nfixa = ts(F(1), nfix, BIGA / BIGB, OP.mult)
     nfix64 = ts(F(1), nfix, 64.0, OP.add)
     nfixm = ts(F(1), nfix, -64.0, OP.add)
     HT = mset(B(224), 0.0)
@@ -286,16 +287,20 @@ def build(rank, n, cores, T, topo):
     lq = sl(landq, 0, 16 * max(rank, 1))
     recv(lq, "r1", sum(count(a, list(range(n - 1, a, -1))) for a in range(rank)), qb, T_REM + (700 if rank < n - 1 else 1300))
 
-    medb = ts(B(128), medi, 128.0, OP.mult)
-    MT = B(2304)
+    MA, MT = B(2304), B(2304)
     tb = ["Y0", "Y1", "Z0", "Z1"]
-    for k in range(4):
-        for r in range(4 * k, 4 * k + 4):
-            mm(bank(tb[k], 128 * (r % 4), 128 * (r % 4) + 128), Sel[r], medb)
-            ops[-1]["boost"] = BOOST - 500.0 * k
-        act(sl(MT, 128 + 512 * k, 640 + 512 * k), bank(tb[k], 0, 512), AF.Identity)
-    cp(sl(MT, 0, 128), sl(MT, 2048, 2176))
-    cp(sl(MT, 2176, 2304), sl(MT, 128, 256))
+    for i, (tab, m) in enumerate(((MA, ts(B(128), ts(I(128), medi, 3, OP.bitwise_and), 128.0, OP.mult)),
+                                  (MT, ts(B(128), medi, 128.0, OP.mult)))):
+        for k in range(4):
+            for r in range(4 * k, 4 * k + 4):
+                mm(bank(tb[k], 128 * (r % 4), 128 * (r % 4) + 128), Sel[r], m)
+                ops[-1]["boost"] = BOOST - 400.0 * k - 1000.0 * i
+            if COPY[4 * i + k] == "S":
+                act(sl(tab, 128 + 512 * k, 640 + 512 * k), bank(tb[k], 0, 512), AF.Identity)
+            else:
+                cp(sl(tab, 128 + 512 * k, 640 + 512 * k), bank(tb[k], 0, 512))
+        cp(sl(tab, 0, 128), sl(tab, 2048, 2176))
+        cp(sl(tab, 2176, 2304), sl(tab, 128, 256))
     kb = cp(B(512), kicki)
     ops[-1]["boost"] = BK
     for i, l in enumerate((ident, Kprev, Klast)):
@@ -322,25 +327,34 @@ def build(rank, n, cores, T, topo):
         a = ts(F(wid(vE)), vE, base, OP.add, -63.0, OP.max) if base is not None else ts(F(wid(vE)), vE, -63.0, OP.max)
         if base is None:
             ops[-1]["rd"].append(lq)
-        ts(uo, a, 63.0, OP.min, fix64, OP.add)
+        ts(uo, a, 63.0, OP.min, 64.0, OP.add)
         cp(yo, tt(F(wid(vE)), uo, xfix, OP.add))
 
-    def scatter3(b, k, yo, u, x, xw, last):
+    def scatter3(b, k, yo, u, xw, before, last):
         w = 16 * k
         for it in range(3):
-            mw = act(B(w), MT, AF.Identity, ind=yo)
-            sgn = act(B(w), MT, AF.Sign, bias=sbias, ind=yo)
-            sm = scan(B(w), sl(d0a, 0, w), mw, 0.0, OP.add, OP.max)
-            ko = cp(U(k), ts(I(k), tt(I(k), sl(sm, 15, w, 16), u, OP.add), 511, OP.bitwise_and))
+            if it == 0:
+                mw = act(B(w), MA, AF.Identity, ind=yo)
+                sgn = act(B(w), MT, AF.Sign, bias=sbias, ind=yo)
+                sm = scan(B(w), sl(d0a, 0, w), mw, 0.0, OP.add, OP.max)
+                ko = ts(U(k), tt(F(k), sl(sm, 15, w, 16), u, OP.add), nfixa, OP.add)
+            else:
+                mw = tt(F(w), MA, u, OP.add, ind=yo)
+                sgn = act(B(w), MT, AF.Sign, bias=sbias, ind=yo)
+                sm = scan(F(w), sl(d0b, 0, w), mw, 0.0, OP.add, OP.max)
+                ko = ts(U(k), sl(sm, 15, w, 16), nfix, OP.add)
             kw = tt(B(w), KT, sgn, OP.mult, ind=ko)
             if it == 2:
                 last(kw)
                 return
             mm(bank("U%d" % b, 0, w), S0f, xw, True, False)
             mm(bank("U%d" % b, 0, w), BOh, kw, False, True)
+            mm(bank("Y%d" % b, 0, w), BOh, kw)
             su = scan(F(w), sl(d0b, 0, w), bank("U%d" % b, 0, w), 0.0, OP.add, OP.max)
             yo = ts(U(k), sl(su, 15, w, 16), nfix64, OP.add)
-            u = tt(F(k), sl(su, 15, w, 16), x, OP.subtract)
+            u = act(B(w), bank("Y%d" % b, 0, w), AF.Identity)
+            if it == 1:
+                before()
 
     def leavers(s, b, c0, w, st):
         Z, Fl = Zs[s], Fs[s]
@@ -357,9 +371,11 @@ def build(rank, n, cores, T, topo):
             else:
                 red(sl(cnt, k), ts(B(w + x), cum, sl(sk, k), OP.is_le, 2.0, OP.mult))
         if b == 0:
-            st["cnt"] = tt(F(4), cnt, offc[s], OP.add)
+            st["cnt"] = ts(F(4), tt(F(4), cnt, offc[s], OP.add), 0.5, OP.mult)
             return None
-        so = ts(U(4), tt(F(4), cnt, st["cnt"], OP.add), 0.5, OP.mult)
+        so = U(4)
+        for k in range(4):
+            ts(sl(so, k), sl(cnt, k), 0.5, OP.mult, sl(st["cnt"], k), OP.add)
         return tt(F(64), sl(Z, 0, c0 + w + 2), adj, OP.add, ind=so)
 
     def exchange(msg, s, lL, lR):
@@ -375,7 +391,7 @@ def build(rank, n, cores, T, topo):
     if rank > 0:
         mm(bank("U1", 0, 16 * rank), BO, lq)
         pre = red(F(1), bank("U1", 0, 16 * rank))
-    xfix = ts(F(16), xf, nfix64, OP.add)
+    xfix = ts(F(16), xf, 64.0, OP.add)
     u0, y0 = F(16), U(16)
     start(vE, pre, xfix, u0, y0)
     Z0 = F(256)
@@ -389,9 +405,11 @@ def build(rank, n, cores, T, topo):
     msg = [None]
     for b in range(2):
         c0 = 128 * b
-        mm(bank("Y%d" % b, 0, 128), LY, sl(Z0, c0, c0 + 128), True, False)
-        mm(bank("Y%d" % b, 0, 128), LP01, sl(dead, c0, c0 + 128), False, False)
         mm(bank("Z%d" % b, 0, 128), LZ, sl(Z0, c0, c0 + 128), True, False)
+
+        def before(b=b, c0=c0):
+            mm(bank("Y%d" % b, 0, 128), LY, sl(Z0, c0, c0 + 128), True, False)
+            mm(bank("Y%d" % b, 0, 128), LP01, sl(dead, c0, c0 + 128), False, False)
 
         def last(kw, b=b, c0=c0):
             if b == 1:
@@ -400,7 +418,7 @@ def build(rank, n, cores, T, topo):
             if b == 0:
                 mm(bank("QQ", c0, c0 + 128), BOh, kw, False, False)
             mm(bank("Z%d" % b, 0, 128), LZm, kw, False, True)
-        scatter3(b, 8, sl(y0, 8 * b, 8 * b + 8), sl(u0, 8 * b, 8 * b + 8), sl(xf, 8 * b, 8 * b + 8), sl(Z0, c0, c0 + 128), last)
+        scatter3(b, 8, sl(y0, 8 * b, 8 * b + 8), sl(u0, 8 * b, 8 * b + 8), sl(Z0, c0, c0 + 128), before, last)
     acc = F(1)
     act(B(256), bank("QQ", 0, 256), AF.Sign, bias=qbias, acc=acc)
 
@@ -423,8 +441,7 @@ def build(rank, n, cores, T, topo):
     qv = sl(sy, 15, 256, 16)
     ho = ts(I(16), qv, ts(F(1), nfix, 4096.0, OP.add), OP.add, 12800.0, OP.min)
     ho = cp(U(16), ts(I(16), ho, 6, OP.arith_shift_right))
-    xx = F(20)
-    yr = tt(sl(xx, 0, 16), qv, ts(F(16), sg, -4096.0, OP.mult, nfixm, OP.add), OP.add)
+    yr = tt(F(16), qv, ts(F(16), sg, -4096.0, OP.mult, nfixm, OP.add), OP.add)
     x2 = ts(F(16), yr, 0.0, OP.max, 2047.0, OP.min)
     v2 = tt(F(16), qfix, xf, OP.subtract)
     if pre is not None:
@@ -446,7 +463,7 @@ def build(rank, n, cores, T, topo):
     for i, (l, r) in enumerate(terms):
         mm(base, l, r, i == 0, i == len(terms) - 1)
     u0, y0 = F(20), U(20)
-    start(vE, base, ts(F(16), x2, nfix64, OP.add), sl(u0, 0, 16), sl(y0, 0, 16))
+    start(vE, base, ts(F(16), x2, 64.0, OP.add), sl(u0, 0, 16), sl(y0, 0, 16))
     ab = B(64)
     Z1 = Zs[0]
     for side, pr in ((0, sl(cs, 0)), (1, preR)):
@@ -459,23 +476,24 @@ def build(rank, n, cores, T, topo):
     mm(bank("U1", 64, 128), Sel[1], ab)
     sa = scan(F(128), sl(d0b, 0, 128), bank("U1", 0, 128), 0.0, OP.add, OP.max)
     ts(sl(y0, 16, 20), sl(sa, 15, 64, 16), nfix64, OP.add)
-    cp(sl(u0, 16, 20), sl(sa, 79, 128, 16))
-    tt(sl(xx, 16, 20), sl(sa, 15, 64, 16), sl(sa, 79, 128, 16), OP.subtract)
+    ts(sl(u0, 16, 20), sl(sa, 79, 128, 16), nfix, OP.add)
     st2 = dict(cum=B(321))
     sy = F(320)
     parts = ((0, K0), (K0, 20))
     for b, (k0, k1) in enumerate(parts):
         c0, w = 16 * k0, 16 * (k1 - k0)
         c1 = min(c0 + w, 256)
-        mm(bank("Y%d" % b, 0, w), LY, sl(Z1, c0, c0 + w), True, False)
-        mm(bank("Y%d" % b, 0, c1 - c0), LP01, sl(dead, c0, c1), False, False)
-        mm(bank("Y%d" % b, 0, c1 - c0), LP01, sl(Fs[0], c0, c1), False, False)
         mm(bank("Z%d" % b, 0, w), LZ, sl(Z1, c0, c0 + w), True, False)
+
+        def before(b=b, c0=c0, c1=c1, w=w):
+            mm(bank("Y%d" % b, 0, w), LY, sl(Z1, c0, c0 + w), True, False)
+            mm(bank("Y%d" % b, 0, c1 - c0), LP01, sl(dead, c0, c1), False, False)
+            mm(bank("Y%d" % b, 0, c1 - c0), LP01, sl(Fs[0], c0, c1), False, False)
 
         def last(kw, b=b, w=w):
             mm(bank("Y%d" % b, 0, w), BOh, kw, False, True)
             mm(bank("Z%d" % b, 0, w), LZm, kw, False, True)
-        scatter3(b, k1 - k0, sl(y0, k0, k1), sl(u0, k0, k1), sl(xx, k0, k1), sl(Z1, c0, c0 + w), last)
+        scatter3(b, k1 - k0, sl(y0, k0, k1), sl(u0, k0, k1), sl(Z1, c0, c0 + w), before, last)
     for b, (k0, k1) in enumerate(parts):
         msg[0] = leavers(1, b, 16 * k0, 16 * (k1 - k0), st2)
     cnt2 = sl(st2["cum"], 318, 320)

from concourse.bass import DstId, RemoteDMATransfer
from concourse.mybir import AluOpType as OP, AxisListType as AX, ActivationFunctionType as AF

POOL = {"pf": ("float32", 11000), "pb": ("bfloat16", 28000), "pi": ("int32", 1600), "pu": ("uint16", 640)}
BANKS = ["U0", "U1", "Y0", "Y1", "Z0", "Z1", "QQ", "MM"]
SCRATCH = {k: ("sbuf", [128, n], d) for k, (d, n) in POOL.items()}
SCRATCH.update({b: ("psum", [128, 512], "float32") for b in BANKS})
NDMA = 12
SEMAPHORES = ["sV", "sS", "sP", "sG", "loc", "r1", "e0", "e7", "eR", "dL1", "dR1", "n2", "dL2", "dR2"] + \
             ["dm%d" % i for i in range(NDMA)]

BIGA, BIGB = 8192.0, 32768.0
SYNC, T_DMA, T_REM, T_CALL = 200.0, 2000.0, 2300.0, 600.0
CYC, PCYC, TRIES = 1.0, 0.7, 24
BOOST, BK, BZ, K0 = 2500.0, 1000.0, 0.0, 12
COPY = "SSSVSSVV"
KS = (3, 3)


def build(rank, n, cores, T, topo):
    ops = []
    top = {k: 0 for k in POOL}

    def new(pool, w):
        a = top[pool]
        top[pool] = a + (w + 15) // 16 * 16
        assert top[pool] <= POOL[pool][1], pool
        return (pool, a, a + w, 1)

    def sl(r, a, b=None, s=1):
        b = a + 1 if b is None else b
        return (r[0], r[1] + a * r[3], r[1] + (b - 1) * r[3] + 1, s * r[3])

    def wid(r):
        return (r[2] - r[1] + r[3] - 1) // r[3]

    def ap(r):
        if not isinstance(r, tuple):
            return r
        return T[r[0]][:, r[1]:r[2]] if r[3] == 1 else T[r[0]][:, r[1]:r[2]:r[3]]

    def bank(b, a, c):
        return (b, a, c, 1)

    def add(eng, fn, rd, wr, dur, **kw):
        o = dict(eng=eng, fn=fn, rd=[r for r in rd if isinstance(r, tuple)], wr=wr, dur=dur, id=len(ops))
        o.update(kw)
        ops.append(o)
        return o

    def two(*rs):
        return all(r[0] in ("pb", "pu") for r in rs)

    def vd(nel, f=1.0):
        return max(64.0, nel * f) * CYC

    def gd(nel, base):
        return base + 1.55 * nel * CYC

    def src(i, ind):
        return ap(i) if ind is None else ap(i).indirect(ap(ind))

    def ts(out, i, s1, o0, s2=None, o1=None, ind=None):
        def fn(e):
            if o1 is None:
                return e.tensor_scalar(ap(out), src(i, ind), ap(s1), None, o0)
            return e.tensor_scalar(ap(out), src(i, ind), ap(s1), ap(s2), o0, o1)
        d = gd(wid(out), 50) if ind else vd(wid(out), 0.5 if two(out, i) else 1.0)
        add("V", fn, [i, s1, s2, ind], [out], d)
        return out

    def tt(out, a, b, o, ind=None):
        d = gd(wid(out), 50) if ind else vd(wid(out), 1.0 if (a[0] in BANKS or b[0] in BANKS) else 2.0)
        add("V", lambda e: e.tensor_tensor(ap(out), src(a, ind), ap(b), o), [a, b, ind], [out], d)
        return out

    def cp(out, i, ind=None):
        d = gd(wid(out), 50) if ind else vd(wid(out), 0.5 if two(out, i) else 1.0)
        add("V", lambda e: e.tensor_copy(ap(out), src(i, ind)), [i, ind], [out], d)
        return out

    def scat(win, off, i):
        add("V", lambda e: e.tensor_copy(ap(win).indirect(ap(off)), ap(i)), [i, off], [win], 50 + 3.5 * wid(i) * CYC)

    def scan(out, a, b, init, o0, o1):
        add("V", lambda e: e.tensor_tensor_scan(ap(out), ap(a), ap(b), ap(init), o0, o1), [a, b, init], [out],
            vd(wid(out), 0.5 if two(out, a, b) else 1.0))
        return out

    def red(out, i):
        add("V", lambda e: e.tensor_reduce(ap(out), ap(i), AX.X, OP.add), [i], [out], vd(wid(i)))
        return out

    def mset(out, c):
        add("V", lambda e: e.memset(ap(out), c), [], [out], vd(wid(out), 0.5 if two(out) else 1.0))
        return out

    def act(out, i, f, bias=None, scale=None, acc=None, ind=None):
        def fn(e):
            kw = {}
            if bias is not None:
                kw["bias"] = ap(bias)
            if scale is not None:
                kw["scale"] = ap(scale)
            if acc is not None:
                kw["accum_out"] = ap(acc)
            return e.activation(ap(out), src(i, ind), f, **kw)
        d = gd(wid(out), 65) if ind else vd(wid(out))
        add("S", fn, [i, bias, scale, ind], [out] + ([acc] if acc else []), d + (25 if acc else 0))
        return out

    def mul(out, i, s):
        return act(out, i, AF.Identity, scale=s)

    grp = [0]
    opened = {}

    def mm(out, l, r, start=True, stop=True):
        if start:
            grp[0] += 1
            opened[out[0]] = grp[0]
        d = max(64, wid(r)) * (4 if l[0] == "pf" else 1) * PCYC
        add("P", lambda e: e.matmul(ap(out), ap(l), ap(r), start, stop), [l, r], [out], d, grp=opened[out[0]])
        return out

    def iota(out, pat, base, cm):
        if out[0] == "pi":
            fn = lambda e: e.iota(ap(out), pat, base, cm)
        else:
            fn = lambda e: e.iota(ap(out), pat, base, cm, allow_small_or_imprecise_dtypes=True)
        add("G", fn, [], [out], 130 + 2 * wid(out) * CYC)
        return out

    def asel(out, i, pat, o, fill, base, cm):
        add("G", lambda e: e.affine_select(ap(out), ap(i), pat, o, fill, base, cm), [i], [out], 170 + 2 * wid(out) * CYC)
        return out

    nd = [0]

    def dma(q, out, i, rd, wr, extra=0.0):
        s = "dm%d" % nd[0]
        nd[0] += 1
        return add(q, lambda e: e.dma_start(out, i), rd, wr, 60.0, lat=T_DMA + extra, dsem=s)

    def plan(a, dsts):
        far = [d for d in dsts if topo.chip(cores[d]) != topo.chip(cores[a])]
        near = [d for d in dsts if d not in far]
        other = [d for d in range(n) if topo.chip(cores[d]) != topo.chip(cores[a])][0]
        leave = topo.engines(cores[a], cores[other])
        out = []
        if far:
            out.append((leave, far))
        if near:
            out.append(([x for x in topo.engines(cores[a], cores[near[0]]) if x not in leave], near))
        return out

    def count(a, dsts):
        return [len(e) for e, ds in plan(a, dsts) if rank in ds][0]

    nloc = [0]

    def send(data, dsts, where):
        tr = []
        for eng, ds in plan(rank, dsts):
            m = sum(1 << x for x in eng)
            ids = [DstId(rid=topo.addr(cores[d])[0], pnc=topo.addr(cores[d])[1]) for d in ds]
            tr.append((ids, m, where(ds[0])[1], [where(d)[0] for d in ds]))
            nloc[0] += len(eng)

        def fn(e):
            return e.remote_dma_fused([RemoteDMATransfer(dst_ids=i, dma_engine_mask=m, remote_sem=T.sem[s], srcs=[ap(data)],
                                                         dsts=[ap(x) for x in ds]) for i, m, s, ds in tr], local_sem=T.sem.loc)
        return add("G", fn, [data], [("sent",) + data[1:]], T_CALL, remote=True)

    def recv(land, sem, cnt, ready, lat):
        return add(None, None, [ready, ("sent",) + ready[1:]], [land], lat, rsem=(sem, cnt))

    F, B, I, U = (lambda w: new("pf", w)), (lambda w: new("pb", w)), (lambda w: new("pi", w)), (lambda w: new("pu", w))
    left, right = (rank + n - 1) % n, (rank + 1) % n

    landq = B(16 * n)
    lande = F(4)
    land1 = F(128)
    landn = B(2)
    FW = F(712)

    xi, vi, wi, li, medi, kicki, zp = I(16), I(16), I(16), I(1), I(128), I(512), I(256)
    dma("Y", ap(wi), T.w[:], [], [wi])
    dma("S", ap(li), T.live[:], [], [li])
    dma("Y", ap(xi), T.x[:], [], [xi])
    dma("S", ap(medi), T.med[:], [], [medi], 200)
    dma("Y", ap(kicki), T.kick[:], [], [kicki], 800)
    dma("S", ap(vi), T.v[:], [], [vi])
    mset(zp, 0)
    for row, t in ((0, T.x), (2, T.w), (3, T.w)):
        dma("Y", T.pi[row:128:16, zp[1]:zp[2]], t[:], [zp], [("zp%d" % row, 0, 1, 1)])

    pint = iota(I(1), [[1, 1]], 0, 1)
    rf = cp(F(1), ts(I(1), pint, 15, OP.bitwise_and))
    g16 = cp(F(1), ts(I(1), pint, 112, OP.bitwise_and))
    jL = ts(F(20), iota(F(20), [[16, 20]], 0, 1), g16, OP.subtract)
    c16 = iota(B(128), [[16, 8], [0, 16]], 0, -1)
    dg = iota(B(128), [[32, 8], [1, 16]], 0, -1)
    t16 = iota(B(16), [[1, 16]], 0, -1)
    negr = ts(F(1), rf, -1.0, OP.mult)
    ng = ts(F(1), g16, -1.0, OP.mult)
    BO = ts(B(128), c16, negr, OP.is_equal)
    EQ = ts(F(16), t16, ng, OP.is_equal)
    Sel = [ts(B(128), c16, float(-r), OP.is_equal) for r in range(16)]
    ident = ts(B(128), dg, g16, OP.is_equal)
    Kprev = ts(B(128), dg, ts(F(1), g16, 1.0, OP.add), OP.is_equal, -1.0, OP.mult)
    Klast = ts(B(128), dg, ts(F(1), g16, -15.0, OP.add), OP.is_equal)
    Tri = asel(B(128), BO, [[1, 128]], OP.is_ge, 0.0, 0, -1)
    BOh = mul(B(128), BO, 0.5)
    S0f = mul(F(128), Sel[0], 1.0)
    d0a = B(16 * K0)
    tt(sl(d0a, 0, 16), ts(F(16), t16, ts(F(1), ng, 1.0, OP.add), OP.is_equal, BIGA, OP.mult),
       ts(F(16), EQ, -4 * BIGA, OP.mult), OP.add)
    w = 16
    while w < 16 * K0:
        k = min(w, 16 * K0 - w)
        mul(sl(d0a, w, w + k), sl(d0a, 0, k), 1.0)
        w += k
    d0b = mul(B(16 * K0), d0a, BIGB / BIGA)
    nfix = ts(F(1), sl(EQ, 15), BIGB, OP.mult, -BIGB, OP.add)
    nfixa = ts(F(1), nfix, BIGA / BIGB, OP.mult)
    nfix64 = ts(F(1), nfix, 64.0, OP.add)
    nfixm = ts(F(1), nfix, -64.0, OP.add)
    HT = mset(B(224), 0.0)
    ts(sl(HT, 17, 33), EQ, -1.0, OP.mult)
    cp(sl(HT, 145, 161), EQ)
    sbias = ts(F(1), rf, -512.0, OP.mult, 64.0, OP.add)
    kbias = ts(F(1), sl(EQ, 0), 128.0, OP.mult)
    jP = ts(F(16), iota(F(16), [[1, 16]], 0, 16), ts(F(1), g16, 16.0, OP.mult), OP.subtract)
    jPu = cp(U(16), jP)
    jW = iota(B(256), [[1, 256]], 0, 0)
    par = iota(B(128), [[0, 64], [-8192, 2]], 4096, 0)
    parBO = asel(B(128), asel(B(128), par, [[-16, 8], [0, 16]], OP.is_ge, 0.0, 0, 1), [[16, 8], [0, 16]], OP.is_ge, 0.0, 15, -1)
    e01 = ts(F(1), rf, 2.0, OP.is_lt)
    LP01 = mul(B(128), parBO, e01)
    LY = asel(F(128), mul(F(128), parBO, sl(EQ, 4)), [[-16, 8], [0, 16]], OP.not_equal, 1.0, 0, 1)
    LZ = mul(F(128), ident, tt(F(1), ts(F(1), rf, 4.0, OP.is_lt), sl(EQ, 1), OP.subtract))
    LQ = mul(F(128), BO, ts(F(1), sl(EQ, 3), 4096.0, OP.mult, sl(EQ, 0), OP.add))
    LQd = mul(B(128), Sel[0], 16384.0)
    LZm = asel(B(128), BOh, [[0, 8], [-1, 16]], OP.is_ge, 0.0, 1, 0)
    S01 = mul(B(128), BO, e01)
    zbias = ts(F(1), e01, -64.0, OP.mult)
    qbias = ts(F(1), rf, -2048.0, OP.mult, 6080.5, OP.add)
    zhi = ts(F(1), sl(EQ, 3), -4194303.0, OP.mult, 4194304.0, OP.add)
    zlo = ts(F(1), zhi, -1.0, OP.mult)
    rodd = cp(F(1), ts(I(1), pint, 1, OP.bitwise_and))
    fsgn = ts(F(1), rodd, 2.0, OP.mult, -1.0, OP.add)
    fth = ts(F(1), rodd, 2175.0, OP.mult, -63.0, OP.add)
    rh = cp(F(1), ts(I(1), pint, 15, OP.bitwise_and, 1, OP.arith_shift_right))
    sk = ts(F(4), sl(jL, 0, 4), rf, OP.subtract)
    sk = ts(F(4), sk, 0.5, OP.mult, rh, OP.add)
    skh = ts(F(4), sk, 0.5, OP.add)
    adj = ts(F(64), sl(par, 0, 64), sl(EQ, 0), OP.mult, 0.5, OP.mult)
    e164 = ts(F(1), sl(EQ, 1), 64.0, OP.mult)

    def coef(pos, neg):
        return tt(F(1), tt(F(1), sl(EQ, pos[0]), sl(EQ, pos[1]), OP.add), tt(F(1), sl(EQ, neg[0]), sl(EQ, neg[1]), OP.add), OP.subtract)

    CL = mul(F(128), BOh, coef((1, 3), (0, 5)))
    CR = mul(F(128), BOh, coef((3, 6), (2, 7)))
    if rank > 0:
        CLn = mul(F(128), CL, -1.0)
    T2 = asel(B(128), asel(B(128), mul(B(128), BO, -1.0), [[-1, 128]], OP.is_gt, 0.0, 0, 1), [[-1, 128]], OP.not_equal, 320.0, 0, 1)
    mset(sl(FW, 320, 580), 0.0)
    mset(sl(FW, 708, 712), 0.0)
    Zs, Fs, offc = [F(322), F(322)], [B(257), B(321)], []
    for s, (w0, w) in enumerate(((128, 256), (16 * K0, 320))):
        ts(sl(Zs[s], w, w + 2), sl(adj, 0, 2), -1.0, OP.mult, sl(EQ, 4), OP.add)
        ts(sl(Fs[s], w), rodd, -128.0, OP.mult, 128.0, OP.add)
        o = F(4)
        for k in range(4):
            mset(sl(o, k), float((w0 if k < KS[0] else 0) + (w + 1 - w0 if k < KS[1] else 0)))
        offc.append(o)

    nf = cp(F(1), li)
    on = ts(F(16), sl(jL, 0, 16), nf, OP.is_lt)
    sg = ts(F(16), wi, -1.0, OP.max, 1.0, OP.min)
    qb = tt(B(16), on, sg, OP.mult)
    if rank < n - 1:
        send(qb, list(range(n - 1, rank, -1)), lambda d: (sl(landq, 16 * rank, 16 * rank + 16), "r1"))
    pre = None
    lq = sl(landq, 0, 16 * max(rank, 1))
    recv(lq, "r1", sum(count(a, list(range(n - 1, a, -1))) for a in range(rank)), qb, T_REM + (700 if rank < n - 1 else 1300))

    MA, MT = B(2304), B(2304)
    tb = ["Y0", "Y1", "Z0", "Z1"]
    for i, (tab, m) in enumerate(((MA, ts(B(128), ts(I(128), medi, 3, OP.bitwise_and), 128.0, OP.mult)),
                                  (MT, ts(B(128), medi, 128.0, OP.mult)))):
        for k in range(4):
            for r in range(4 * k, 4 * k + 4):
                mm(bank(tb[k], 128 * (r % 4), 128 * (r % 4) + 128), Sel[r], m)
                ops[-1]["boost"] = BOOST - 400.0 * k - 1000.0 * i
            if COPY[4 * i + k] == "S":
                act(sl(tab, 128 + 512 * k, 640 + 512 * k), bank(tb[k], 0, 512), AF.Identity)
            else:
                cp(sl(tab, 128 + 512 * k, 640 + 512 * k), bank(tb[k], 0, 512))
        cp(sl(tab, 0, 128), sl(tab, 2048, 2176))
        cp(sl(tab, 2176, 2304), sl(tab, 128, 256))
    kb = cp(B(512), kicki)
    ops[-1]["boost"] = BK
    for i, l in enumerate((ident, Kprev, Klast)):
        mm(bank("QQ", 0, 512), l, kb, i == 0, i == 2)
    KT = act(B(512), bank("QQ", 0, 512), AF.Identity, bias=kbias)

    def field(ho, q, v):
        h = F(2)
        S0 = act(B(256), sl(HT, 16, 224), AF.Identity, acc=sl(h, 0), ind=ho)
        S1 = act(B(256), sl(HT, 0, 208), AF.Identity, acc=sl(h, 1), ind=ho)
        hb = cp(B(2), h)
        mm(bank("MM", 0, 2), Tri, hb, True, False)
        mm(bank("MM", 1, 2), BO, sl(hb, 0), False, True)
        l0 = ts(B(128), BO, bank("MM", 0, 1), OP.mult)
        l1 = ts(B(128), BO, bank("MM", 1, 2), OP.mult)
        mm(bank("U0", 0, 256), l0, S0, True, False)
        mm(bank("U0", 0, 256), l1, S1, False, True)
        sc = F(256)
        for a in (0, 128):
            scan(sl(sc, a, a + 128), sl(d0b, 0, 128), bank("U0", a, a + 128), 0.0, OP.add, OP.max)
        return tt(F(16), tt(F(16), sl(sc, 15, 256, 16), q, OP.mult), v, OP.add), hb

    def start(vE, base, xfix, uo, yo):
        a = ts(F(wid(vE)), vE, base, OP.add, -63.0, OP.max) if base is not None else ts(F(wid(vE)), vE, -63.0, OP.max)
        if base is None:
            ops[-1]["rd"].append(lq)
        ts(uo, a, 63.0, OP.min, 64.0, OP.add)
        cp(yo, tt(F(wid(vE)), uo, xfix, OP.add))

    def scatter3(b, k, yo, u, xw, before, last):
        w = 16 * k
        for it in range(3):
            if it == 0:
                mw = act(B(w), MA, AF.Identity, ind=yo)
                sgn = act(B(w), MT, AF.Sign, bias=sbias, ind=yo)
                sm = scan(B(w), sl(d0a, 0, w), mw, 0.0, OP.add, OP.max)
                ko = ts(U(k), tt(F(k), sl(sm, 15, w, 16), u, OP.add), nfixa, OP.add)
            else:
                mw = tt(F(w), MA, u, OP.add, ind=yo)
                sgn = act(B(w), MT, AF.Sign, bias=sbias, ind=yo)
                sm = scan(F(w), sl(d0b, 0, w), mw, 0.0, OP.add, OP.max)
                ko = ts(U(k), sl(sm, 15, w, 16), nfix, OP.add)
            kw = tt(B(w), KT, sgn, OP.mult, ind=ko)
            if it == 2:
                last(kw)
                return
            mm(bank("U%d" % b, 0, w), S0f, xw, True, False)
            mm(bank("U%d" % b, 0, w), BOh, kw, False, True)
            mm(bank("Y%d" % b, 0, w), BOh, kw)
            su = scan(F(w), sl(d0b, 0, w), bank("U%d" % b, 0, w), 0.0, OP.add, OP.max)
            yo = ts(U(k), sl(su, 15, w, 16), nfix64, OP.add)
            u = act(B(w), bank("Y%d" % b, 0, w), AF.Identity)
            if it == 1:
                before()

    def leavers(s, b, c0, w, st):
        Z, Fl = Zs[s], Fs[s]
        x = 1 if b else 0
        ts(sl(Fl, c0, c0 + w), bank("Y%d" % b, 0, w), fsgn, OP.mult, fth, OP.is_ge)
        cum = sl(st["cum"], c0, c0 + w + x)
        f = sl(Fl, c0, c0 + w + x)
        scan(cum, f, f, sl(st["cum"], c0 - 1) if b else 0.0, OP.add, OP.max)
        act(sl(Z, c0, c0 + w), bank("Z%d" % b, 0, w), AF.Identity, bias=zbias)
        cnt = F(4)
        for k in range(4):
            if k < KS[b]:
                act(B(w + x), cum, AF.Sign, bias=sl(skh, k), scale=-1.0, acc=sl(cnt, k))
            else:
                red(sl(cnt, k), ts(B(w + x), cum, sl(sk, k), OP.is_le, 2.0, OP.mult))
        if b == 0:
            st["cnt"] = ts(F(4), tt(F(4), cnt, offc[s], OP.add), 0.5, OP.mult)
            return None
        so = U(4)
        for k in range(4):
            ts(sl(so, k), sl(cnt, k), 0.5, OP.mult, sl(st["cnt"], k), OP.add)
        return tt(F(64), sl(Z, 0, c0 + w + 2), adj, OP.add, ind=so)

    def exchange(msg, s, lL, lR):
        names = ("dL%d" % s, "dR%d" % s)
        send(msg, [right, left], lambda d: (lL, names[0]) if d == right else (lR, names[1]))
        recv(lL, names[0], count(left, [rank, (left + n - 1) % n]), msg, T_REM)
        recv(lR, names[1], count(right, [(right + 1) % n, rank]), msg, T_REM)

    xf = cp(F(16), xi)
    ho = cp(U(16), tt(F(16), ts(I(16), xi, 6, OP.arith_shift_right), ts(F(16), qb, 64.0, OP.mult, 65.0, OP.add), OP.add))
    qfix = ts(F(16), qb, nfix, OP.mult)
    vE, _ = field(ho, qb, tt(F(16), qfix, vi, OP.add))
    if rank > 0:
        mm(bank("U1", 0, 16 * rank), BO, lq)
        pre = red(F(1), bank("U1", 0, 16 * rank))
    xfix = ts(F(16), xf, 64.0, OP.add)
    u0, y0 = F(16), U(16)
    start(vE, pre, xfix, u0, y0)
    Z0 = F(256)
    add("V", lambda e: e.tensor_scalar(ap(Z0), ap(zp).indirect(ap(jPu)), ap(zlo), ap(zhi), OP.max, OP.min),
        [zp, jPu, zlo, zhi, ("zp0", 0, 1, 1), ("zp2", 0, 1, 1), ("zp3", 0, 1, 1)], [Z0], gd(256, 50), boost=BZ)
    dead = ts(B(256), jW, nf, OP.is_ge)
    mm(bank("QQ", 0, 256), LQ, Z0, True, False)
    mm(bank("QQ", 0, 256), LQd, dead, False, False)
    st1 = dict(cum=B(257))
    sy = F(256)
    msg = [None]
    for b in range(2):
        c0 = 128 * b
        mm(bank("Z%d" % b, 0, 128), LZ, sl(Z0, c0, c0 + 128), True, False)

        def before(b=b, c0=c0):
            mm(bank("Y%d" % b, 0, 128), LY, sl(Z0, c0, c0 + 128), True, False)
            mm(bank("Y%d" % b, 0, 128), LP01, sl(dead, c0, c0 + 128), False, False)

        def last(kw, b=b, c0=c0):
            if b == 1:
                mm(bank("QQ", c0, c0 + 128), BOh, kw, False, True)
            mm(bank("Y%d" % b, 0, 128), BOh, kw, False, True)
            if b == 0:
                mm(bank("QQ", c0, c0 + 128), BOh, kw, False, False)
            mm(bank("Z%d" % b, 0, 128), LZm, kw, False, True)
        scatter3(b, 8, sl(y0, 8 * b, 8 * b + 8), sl(u0, 8 * b, 8 * b + 8), sl(Z0, c0, c0 + 128), before, last)
    acc = F(1)
    act(B(256), bank("QQ", 0, 256), AF.Sign, bias=qbias, acc=acc)

    def edst(a):
        return [d for d in range(n) if d != a] if a in (0, n - 1) else [a - 1]

    def ecol(a):
        return (0, "e0") if a == 0 else (1, "e7") if a == n - 1 else (2, "eR")
    send(acc, edst(rank), lambda d: (sl(lande, ecol(rank)[0]), ecol(rank)[1]))
    got = {rank: acc}
    for a in sorted({0, n - 1, right} - {rank}):
        got[a] = sl(lande, ecol(a)[0])
        recv(got[a], ecol(a)[1], count(a, edst(a)), acc, T_REM + (700 if a in (0, n - 1) else 0))
    for b in range(2):
        msg[0] = leavers(0, b, 128 * b, 128, st1)
    exchange(msg[0], 1, sl(land1, 0, 64), sl(land1, 64, 128))
    for b in range(2):
        scan(sl(sy, 128 * b, 128 * b + 128), sl(d0b, 0, 128), bank("QQ", 128 * b, 128 * b + 128), 0.0, OP.add, OP.max)

    qv = sl(sy, 15, 256, 16)
    ho = ts(I(16), qv, ts(F(1), nfix, 4096.0, OP.add), OP.add, 12800.0, OP.min)
    ho = cp(U(16), ts(I(16), ho, 6, OP.arith_shift_right))
    yr = tt(F(16), qv, ts(F(16), sg, -4096.0, OP.mult, nfixm, OP.add), OP.add)
    x2 = ts(F(16), yr, 0.0, OP.max, 2047.0, OP.min)
    v2 = tt(F(16), qfix, xf, OP.subtract)
    if pre is not None:
        v2 = ts(F(16), v2, pre, OP.add)
    e31 = mm(bank("U1", 0, 1), CL, got[right])
    v2 = tt(F(16), tt(F(16), v2, yr, OP.add), ts(F(16), x2, 1984.0, OP.is_ge, e31, OP.mult), OP.add)
    vE, hb = field(ho, qb, v2)
    mm(bank("MM", 2, 3), Sel[0], sl(hb, 0))
    mm(bank("MM", 3, 4), BO, sl(hb, 0), True, False)
    mm(bank("MM", 3, 4), BO, sl(hb, 1), False, True)
    if pre is not None:
        cs = ts(F(2), bank("MM", 2, 4), pre, OP.add, sl(EQ, 1), OP.mult)
    else:
        cs = ts(F(2), bank("MM", 2, 4), sl(EQ, 1), OP.mult)
    preR = tt(F(1), sl(cs, 1), sl(adj, 1), OP.add)
    preR = ts(F(1), e31, sl(EQ, 1), OP.mult, preR, OP.add)
    base = bank("QQ", 0, 1)
    terms = [(CR, got[n - 1])] if rank == 0 else [(CL, acc), (CR, got[n - 1]), (CLn, got[0])]
    for i, (l, r) in enumerate(terms):
        mm(base, l, r, i == 0, i == len(terms) - 1)
    u0, y0 = F(20), U(20)
    start(vE, base, ts(F(16), x2, 64.0, OP.add), sl(u0, 0, 16), sl(y0, 0, 16))
    ab = B(64)
    Z1 = Zs[0]
    for side, pr in ((0, sl(cs, 0)), (1, preR)):
        a = sl(land1, 64 * side + 1 - side, 64 * side + 64, 2)
        ecolumn = ts(F(1), base, sl(EQ, 1), OP.mult, pr, OP.add)
        t = ts(F(32), a, ecolumn, OP.add, -63.0, OP.max)
        ts(sl(ab, 32 * side, 32 * side + 32), t, 63.0, OP.min, e164, OP.add)
        act(sl(Z1, 256 + 32 * side, 288 + 32 * side), a, AF.Identity)
    mm(bank("U1", 0, 64), S01, ab)
    mm(bank("U1", 64, 128), Sel[1], ab)
    sa = scan(F(128), sl(d0b, 0, 128), bank("U1", 0, 128), 0.0, OP.add, OP.max)
    ts(sl(y0, 16, 20), sl(sa, 15, 64, 16), nfix64, OP.add)
    ts(sl(u0, 16, 20), sl(sa, 79, 128, 16), nfix, OP.add)
    st2 = dict(cum=B(321))
    sy = F(320)
    parts = ((0, K0), (K0, 20))
    for b, (k0, k1) in enumerate(parts):
        c0, w = 16 * k0, 16 * (k1 - k0)
        c1 = min(c0 + w, 256)
        mm(bank("Z%d" % b, 0, w), LZ, sl(Z1, c0, c0 + w), True, False)

        def before(b=b, c0=c0, c1=c1, w=w):
            mm(bank("Y%d" % b, 0, w), LY, sl(Z1, c0, c0 + w), True, False)
            mm(bank("Y%d" % b, 0, c1 - c0), LP01, sl(dead, c0, c1), False, False)
            mm(bank("Y%d" % b, 0, c1 - c0), LP01, sl(Fs[0], c0, c1), False, False)

        def last(kw, b=b, w=w):
            mm(bank("Y%d" % b, 0, w), BOh, kw, False, True)
            mm(bank("Z%d" % b, 0, w), LZm, kw, False, True)
        scatter3(b, k1 - k0, sl(y0, k0, k1), sl(u0, k0, k1), sl(Z1, c0, c0 + w), before, last)
    for b, (k0, k1) in enumerate(parts):
        msg[0] = leavers(1, b, 16 * k0, 16 * (k1 - k0), st2)
    cnt2 = sl(st2["cum"], 318, 320)
    send(cnt2, [right], lambda d: (landn, "n2"))
    recv(landn, "n2", count(left, [rank]), cnt2, T_REM)
    exchange(msg[0], 2, sl(FW, 580, 644), sl(FW, 644, 708))

    for b, (k0, k1) in enumerate(parts):
        w = 16 * (k1 - k0)
        scan(sl(sy, 16 * k0, 16 * k1), sl(d0b, 0, w), bank("Y%d" % b, 0, w), 0.0, OP.add, OP.max)
    yr = ts(F(20), sl(sy, 15, 320, 16), nfixm, OP.add)
    stay = tt(B(20), ts(F(20), yr, 0.0, OP.max, 2047.0, OP.min), yr, OP.is_equal)
    inc = scan(B(20), stay, stay, 0.0, OP.add, OP.max)
    mm(bank("U0", 0, 20), BO, inc, True, False)
    mm(bank("U0", 0, 20), T2, stay, False, True)
    ns = mm(bank("MM", 0, 1), BO, sl(inc, 19))
    pos = cp(U(20), tt(F(20), bank("U0", 0, 20), jL, OP.max))
    scat(sl(FW, 0, 577), pos, sl(Zs[1], 0, 320))
    t = ts(F(16), jP, ns, OP.subtract)
    A = tt(F(16), ts(F(16), t, 2.0, OP.mult, 261.0, OP.add), ts(F(16), t, 0.0, OP.is_lt, -4096.0, OP.mult), OP.add)
    j1 = ts(F(16), jP, 1.0, OP.add)
    nl = mm(bank("U1", 0, 1), Sel[1], sl(landn, 1))
    s2 = ts(F(1), nl, -2.0, OP.mult, 63.0, OP.add)
    c = tt(F(16), A, ts(F(16), t, nl, OP.is_ge, s2, OP.mult), OP.add)
    fo = ts(U(16), tt(F(16), c, j1, OP.max), 388.0, OP.min)
    FO = F(256)
    win = sl(FW, 320, 712)
    cp(sl(FO, 0, 128), win, ind=sl(fo, 0, 8))
    act(sl(FO, 128, 256), win, AF.Identity, ind=sl(fo, 8, 16))
    for row, q, t in ((0, "Y", T.yx), (1, "S", T.yv), (2, "Y", T.yw)):
        dma(q, t[:], T.pf[row:128:16, FO[1]:FO[2]], [FO], [])
    return ops, nloc[0]


def depend(ops):
    hist = {}
    for o in ops:
        d = set()
        for kind, regs in ((0, o["rd"]), (1, o["wr"])):
            for r in regs:
                for (p, k2, a, b) in hist.get(r[0], []):
                    if p is o:
                        continue
                    if r[0] in BANKS:
                        hit = kind or k2 or p["eng"] != o["eng"]
                    else:
                        hit = (kind or k2) and a < r[2] and r[1] < b
                    if hit:
                        d.add(p["id"])
        o["dep"] = d
        for kind, regs in ((0, o["rd"]), (1, o["wr"])):
            if o["eng"] is None and kind == 0:
                continue
            for r in regs:
                hist.setdefault(r[0], []).append((o, kind, r[1], r[2]))


def loose(p, o):
    if p["eng"] != "P" or o["eng"] != "P":
        return False
    a, b = p["wr"][0], o["wr"][0]
    return p["grp"] == o["grp"] or a[2] <= b[1] or b[2] <= a[1]


def place(ops, key, back):
    pre, post = ("succ", "dep") if back else ("dep", "succ")
    busy = {e: [] for e in "VSPGY"}
    left = [len(o[pre]) for o in ops]
    start = [0.0] * len(ops)
    cand = [o["id"] for o in ops if not o[pre]]
    while cand:
        i = max(cand, key=lambda j: key[j])
        cand.remove(i)
        o = ops[i]
        if back:
            t = o["tot"] - o["dur"] + max([start[d] + ops[d]["dur"] - (SYNC if i in ops[d]["loose"] else 0.0) for d in o[pre]] + [0.0])
        else:
            t = max([start[d] + ops[d]["tot"] - (SYNC if d in o["loose"] else 0.0) for d in o[pre]] + [0.0])
        if o["eng"] is not None:
            l = busy[o["eng"]]
            k = 0
            while k < len(l) and l[k][0] < t + o["dur"]:
                t = max(t, l[k][1])
                k += 1
            l.insert(k, (t, t + o["dur"]))
        start[i] = t
        for s in o[post]:
            left[s] -= 1
            if left[s] == 0:
                cand.append(s)
    return start


def schedule(ops):
    for o in ops:
        o["succ"] = []
        o["tot"] = o["dur"] + o.get("lat", 0.0) + SYNC
        o["loose"] = {d for d in o["dep"] if loose(ops[d], o)}
    for o in ops:
        for d in o["dep"]:
            ops[d]["succ"].append(o["id"])
    for o in reversed(ops):
        o["pr"] = o["tot"] + o.get("boost", 0.0) + max([ops[s]["pr"] for s in o["succ"]] + [0.0])
    best, seed = None, 12345
    for trial in range(TRIES):
        key = []
        for o in ops:
            seed = (seed * 1103515245 + 12345) % 2147483648
            key.append(o["pr"] + (seed / 2147483648.0) * 100.0 * (trial % 8))
        for turn in range(4):
            start = place(ops, key, False)
            end = [start[o["id"]] + o["tot"] for o in ops]
            if best is None or max(end) < best[0]:
                best = (max(end), start, end)
            rev = place(ops, end, True)
            key = [rev[o["id"]] + o["dur"] for o in ops]
    order = {e: [] for e in "VSPGY"}
    for o in ops:
        o["start"], o["end"] = best[1][o["id"]], best[2][o["id"]]
    for o in sorted(ops, key=lambda o: (o["start"], o["id"])):
        if o["eng"] is not None:
            order[o["eng"]].append(o)
    return order


def emit(g, T, ops, order, nloc):
    queue = {"V": g.vector, "S": g.scalar, "P": g.tensor, "G": g, "Y": g.sync}

    def waits_on(o):
        return [ops[d] for d in o["dep"] if d not in o["loose"] and ops[d].get("rsem", (0, 1))[1] > 0 and not ops[d].get("remote")]
    seq = sorted([o for o in ops if o["eng"] is not None], key=lambda o: (o["start"], o["id"]))
    pos = {}
    for e, l in order.items():
        for i, o in enumerate(l):
            pos[o["id"]] = i
    know = {e: {} for e in order}
    for o in seq:
        k = know[o["eng"]]
        need = []
        ps = sorted(waits_on(o), key=lambda p: -p["end"])
        for p in ps:
            key = p["rsem"][0] if p["eng"] is None else p["dsem"] if "dsem" in p else p["eng"]
            val = 0 if (p["eng"] is None or "dsem" in p) else pos[p["id"]]
            if k.get(key, -1) >= val:
                continue
            need.append(p)
            p["inc"] = True
            k[key] = val
            for kk, vv in p.get("know", {}).items():
                if k.get(kk, -1) < vv:
                    k[kk] = vv
        o["need"] = need
        o["know"] = dict(k)
    for e, l in order.items():
        c = 0
        for o in l:
            if "dsem" not in o and o.get("inc"):
                c += 1
                o["val"] = c
    for o in seq:
        q = queue[o["eng"]]
        for p in o["need"]:
            if p["eng"] is None:
                q.wait_ge(T.sem[p["rsem"][0]], p["rsem"][1])
            elif "dsem" in p:
                q.wait_ge(T.sem[p["dsem"]], 16)
            else:
                q.wait_ge(T.sem["s" + p["eng"]], p["val"])
        ins = o["fn"](q)
        if "dsem" in o:
            ins.then_inc(T.sem[o["dsem"]], 16)
        elif o.get("inc"):
            ins.then_inc(T.sem["s" + o["eng"]], 1)
    g.wait_ge(T.sem.loc, nloc)
    for o in seq:
        if "dsem" in o and not o.get("inc"):
            g.wait_ge(T.sem[o["dsem"]], 16)


def rank_program(g, core, T, topo):
    rank = T.rank_of(core)
    if rank is None:
        return
    cores = list(T.cores)
    ops, nloc = build(rank, len(cores), cores, T, topo)
    depend(ops)
    order = schedule(ops)
    emit(g, T, ops, order, nloc)
